import numpy as np
import ml_dtypes


def mxq(x, axis, fmt="e4m3"):
    dtype, down = {"e4m3": (ml_dtypes.float8_e4m3fn, 7), "e5m2": (ml_dtypes.float8_e5m2, 14)}[fmt]
    v = np.moveaxis(np.asarray(x, np.float32).astype(ml_dtypes.bfloat16).astype(np.float64), axis, -1)
    blocks = v.reshape(v.shape[:-1] + (-1, 32))
    amax = np.abs(blocks).max(-1, keepdims=True)
    byte = np.maximum(np.where(amax > 0, np.frexp(amax)[1] - 1 + 127, 0) - down, 1)
    scale = np.exp2(byte - 127.0)
    codes = (blocks / scale).astype(np.float32).astype(dtype).astype(np.float64)
    return np.moveaxis((codes * scale).reshape(v.shape), -1, axis)


WIDE = False


def mx_kscale(k):
    if not WIDE:
        return np.ones(k)
    levels = np.array([10, -10, 5, -5, 0])
    if k % 512:
        return np.exp2(np.random.permutation(np.resize(levels, k // 32))).repeat(32)
    a = np.empty((k // 512, 16))
    for p in range(k // 512):
        a[p, :8] = np.random.permutation(np.resize(levels, 8))
        for g in range(8):
            far = levels[np.abs(levels - a[p, g]) >= 10]
            a[p, g + 8] = far[np.random.randint(len(far))]
    return np.exp2(a.ravel()).repeat(32)


def f64(x):
    return np.asarray(x).astype(np.float64)


def striped(idx):
    return np.tile(idx.reshape(-1, 16).T, (8, 1)).astype(np.uint16)


def unstriped(offs):
    return offs[:16].T.reshape(-1).astype(np.int64)


def pack_weight(w):
    k, n = w.shape
    w = f64(np.asarray(w, np.float32).astype(ml_dtypes.bfloat16)).reshape(k // 32, 32, n)
    amax = np.abs(w).max(1)
    byte = np.clip(np.where(amax > 0, np.frexp(amax)[1] - 1 + 127 - 7, 1), 1, 254)
    scaled = (w * np.exp2(127.0 - byte)[:, None, :]).reshape(k, n).astype(np.float32)
    words = np.ascontiguousarray(scaled.reshape(k // 512, 128, 4, n).transpose(0, 1, 3, 2)).astype(ml_dtypes.float8_e4m3fn).view(np.uint8)
    return words, np.ascontiguousarray(byte.astype(np.uint8).reshape(k // 512, 16, n))


def unpack_weight(words, scales):
    g, p, n, _ = words.shape
    vals = np.ascontiguousarray(words).view(ml_dtypes.float8_e4m3fn).astype(np.float64) * np.repeat(np.exp2(scales.astype(np.float64) - 127.0), 8, axis=1)[..., None]
    return vals.transpose(0, 1, 3, 2).reshape(g * 512, n)


K, T, S, D, N, H, V, U = 512, 2048, 1024, 4, 128, 512, 256, 512


def setup_inputs():
    n = np.random.standard_normal
    s = mx_kscale(K)[:, None]
    u = mx_kscale(H)
    packed_xT = pack_weight(n((K, T)) * s)
    return {
        "x_words": packed_xT[0],
        "x_scales": packed_xT[1],
        "w1": (n((K, H)) / np.sqrt(K) / s).astype(np.float32),
        "w2": (n((K, H)) / np.sqrt(K) / s).astype(np.float32),
        "qry": (n((H, U))).astype(np.float32),
        "unit": (np.random.uniform(0.6, 1.4, (H, 1)) * u[:, None]).astype(np.float32),
        "w3": (n((H, N)) / np.sqrt(H) / u[:, None]).astype(np.float32),
        "offs": striped(np.random.permutation(T)[:S]),
        "rdr": striped(np.random.permutation(np.concatenate([np.arange(V), np.random.randint(0, V, U - V)]))),
    }


def reference(x_words, x_scales, w1, w2, qry, unit, w3, offs, rdr):
    xq = unpack_weight(x_words, x_scales)[:, unstriped(offs)]
    y = mxq(f64(w1), 0, "e4m3").T @ xq
    ay = np.abs(y)
    scl = ay.reshape(len(ay), -1, D).max(axis=2) + 0.2
    sr = scl[:, unstriped(rdr)]
    sq_ = sr * f64(qry)
    lev = y / np.repeat(scl, D, axis=1)
    yz = mxq(f64(w2), 0, "e4m3").T @ xq
    zero = yz.reshape(len(yz), -1, D).mean(axis=2)
    lz = lev * np.repeat(zero, D, axis=1)
    dq = lz.reshape(len(lz), -1, D).sum(axis=2)
    dr = dq[:, unstriped(rdr)]
    hid = f64(unit) * (sq_ + dr)
    return mxq(f64(w3), 0, "e4m3").T @ mxq(hid, 0, "e4m3")

@@ -1,0 +1,202 @@
+from contextlib import ExitStack
+
+import concourse.mybir as mybir
+
+K, T, S, D, N, H, V, U = 512, 2048, 1024, 4, 128, 512, 256, 512
+FLOPS = 2 * K * H * S * 2 + 2 * H * N * U
+
+F32 = mybir.dt.float32
+BF16 = mybir.dt.bfloat16
+I32 = mybir.dt.int32
+U32 = mybir.dt.uint32
+U16 = mybir.dt.uint16
+U8 = mybir.dt.uint8
+FP8X4 = mybir.dt.float8_e4m3fn_x4
+ALU = mybir.AluOpType
+ACT = mybir.ActivationFunctionType
+AX = mybir.AxisListType
+
+P = 128
+PACK = 4
+BANK = 512
+SUM_ON_PE = (2,3,)
+
+
+def tile_picked_ywvres_read_p_kernel(
+    tc, x_words, x_scales, w1, w2, qry, unit, w3, offs, rdr, out
+):
+    nc = tc.nc
+    with ExitStack() as ctx:
+        lists = ctx.enter_context(tc.tile_pool(name="lists", bufs=1))
+        keep = ctx.enter_context(tc.tile_pool(name="keep", bufs=1))
+        work = ctx.enter_context(tc.tile_pool(name="work", bufs=2))
+        psum = ctx.enter_context(tc.psum_pool(name="psum", bufs=1))
+
+        offs_sb = lists.tile([P, S // 16], U16, name="offs_sb")
+        rdr_sb = lists.tile([P, U // 16], U16, name="rdr_sb")
+        nc.sync.dma_start(offs_sb[:], offs)
+
+        def load_half(w, c, name):
+            raw = keep.tile([P, PACK, H // 2], F32, name="%s_raw%d" % (name, c), align_bytes=64)
+            nc.sync.dma_start(
+                raw[:], w.rearrange("(p j) c -> p j c", j=PACK)[:, :, c * (H // 2) : (c + 1) * (H // 2)]
+            )
+            return raw
+
+        w1_raw = [load_half(w1, 0, "w1")]
+        xs_all = keep.tile([P, T], U8, name="xs_all", align_bytes=64)
+        nc.vector.memset(xs_all[:].bitcast(I32), 0)
+        for q in range(4):
+            nc.sync.dma_start(
+                xs_all[32 * q : 32 * q + 4, :].bitcast(I32),
+                x_scales[0, 4 * q : 4 * q + 4, :].bitcast(I32),
+            )
+        xw_all = keep.tile([P, T], I32, name="xw_all", align_bytes=64)
+        nc.sync.dma_start(xw_all[:], x_words[0].rearrange("p c r -> p (c r)").bitcast(I32))
+        w1_raw.append(load_half(w1, 1, "w1"))
+        w2_raw = [load_half(w2, c, "w2") for c in range(2)]
+        unit_sb = keep.tile([P, PACK], F32, name="unit_sb")
+        nc.sync.dma_start(unit_sb[:], unit.rearrange("(p t) o -> p (t o)", t=PACK))
+        nc.sync.dma_start(rdr_sb[:], rdr)
+        qry_sb = []
+        for c in range(2):
+            qt = keep.tile([P, 2, U], F32, name="qry%d" % c, align_bytes=64)
+            nc.sync.dma_start(qt[:], qry.rearrange("(p t) r -> p t r", t=PACK)[:, 2 * c : 2 * c + 2, :])
+            qry_sb.append(qt)
+        w3_raw = keep.tile([P, PACK, N], F32, name="w3_raw", align_bytes=64)
+        nc.sync.dma_start(w3_raw[:], w3.rearrange("(p j) n -> p j n", j=PACK))
+
+        xs = keep.tile([P, S], U8, name="xs", align_bytes=64)
+        nc.vector.tensor_copy(xs[:], xs_all[:].indirect(offs_sb[:]))
+        xw = keep.tile([P, S], U32, name="xw", align_bytes=64)
+        for h in range(2):
+            nc.vector.tensor_copy(
+                xw[:, h * BANK : (h + 1) * BANK],
+                xw_all[:].bitcast(U32).indirect(offs_sb[:, h * 32 : (h + 1) * 32]),
+            )
+
+        def round_weight(halves, name):
+            grouped = keep.tile([P, H * PACK], BF16, name=name + "_bf", align_bytes=64)
+            view = grouped[:].rearrange("p (t m j) -> p m j t", t=PACK, j=PACK)
+            for c in range(2):
+                nc.scalar.copy(
+                    view[:, c * 64 : (c + 1) * 64, :, :],
+                    halves[c][:].rearrange("p j (m t) -> p m j t", t=PACK),
+                )
+            return grouped
+
+        def quantize(grouped, width, name):
+            codes = keep.tile([P, width], U32, name=name + "_codes", align_bytes=64)
+            scales = keep.tile([P, width], U8, name=name + "_scales", align_bytes=64)
+            nc.vector.quantize_mx(out=codes[:].bitcast(FP8X4), scales=scales[:], in_=grouped[:])
+            return codes, scales
+
+        w1_codes, w1_scales = quantize(round_weight(w1_raw, "w1"), H, "w1")
+
+        xs_d = keep.tile([P, S], U8, name="xs_d", align_bytes=64)
+        nc.vector.tensor_copy(
+            xs_d[:].rearrange("p (d v) -> p d v", d=D), xs[:].rearrange("p (v d) -> p d v", d=D)
+        )
+        xw_d = keep.tile([P, S], U32, name="xw_d", align_bytes=64)
+        nc.vector.tensor_copy(
+            xw_d[:].rearrange("p (d c i) -> p c d i", d=D, i=4),
+            xw[:].rearrange("p (c i d) -> p c d i", d=D, i=4),
+        )
+        w2_codes, w2_scales = quantize(round_weight(w2_raw, "w2"), H, "w2")
+
+        unit_q = keep.tile([P, PACK], F32, name="unit_q")
+        nc.vector.tensor_scalar(unit_q[:], unit_sb[:], 1.0 / D, None, ALU.mult)
+        unit_f = keep.tile([P, PACK], F32, name="unit_f")
+        nc.vector.tensor_scalar(unit_f[:], unit_sb[:], 0.2, None, ALU.mult)
+
+        def mx(acc, codes, scales, t, mw, ms, cols, start, stop):
+            nc.tensor.matmul_mx(
+                out=acc,
+                lhsT=codes[:, t * P : (t + 1) * P].bitcast(FP8X4),
+                lhsT_scale=scales[:, t * P : (t + 1) * P],
+                rhs=mw[:, cols].bitcast(FP8X4),
+                rhs_scale=ms[:, cols],
+                start=start,
+                stop=stop,
+            )
+
+        RH = U // 2
+        prod = [keep.tile([P, PACK, RH], F32, name="prod%d" % r, align_bytes=64) for r in range(2)]
+        shift = [keep.tile([P, PACK, RH], F32, name="shift%d" % r, align_bytes=64) for r in range(2)]
+
+        for t in range(PACK):
+            ay = work.tile([P, D, V], F32, name="ay")
+            ysum = None
+            if t not in SUM_ON_PE:
+                ysum = work.tile([P, V], F32, name="ysum")
+            for h in range(2):
+                y = psum.tile([P, BANK], F32, name="y", bufs=4)
+                mx(y[:], w1_codes, w1_scales, t, xw, xs, slice(h * BANK, (h + 1) * BANK), True, True)
+                nc.scalar.activation(
+                    ay[:, :, h * P : (h + 1) * P], y[:].rearrange("p (v d) -> p d v", d=D), ACT.Abs
+                )
+                if ysum is not None:
+                    nc.vector.tensor_reduce(
+                        ysum[:, h * P : (h + 1) * P], y[:].rearrange("p (v d) -> p v d", d=D), AX.X, ALU.add
+                    )
+            zs = psum.tile([P, BANK], F32, name="zs", bufs=2)
+            for d in range(D):
+                mx(zs[:, 0:V], w2_codes, w2_scales, t, xw_d, xs_d, slice(d * V, (d + 1) * V), d == 0, d == D - 1)
+            if ysum is None:
+                for d in range(D):
+                    mx(zs[:, V : 2 * V], w1_codes, w1_scales, t, xw_d, xs_d, slice(d * V, (d + 1) * V), d == 0, d == D - 1)
+
+            wa = keep.tile([P, 3 * V], F32, name="wa%d" % t)
+            wb = keep.tile([P, 3 * V], F32, name="wb%d" % t)
+            nc.vector.tensor_tensor(
+                wa[:, V : 3 * V],
+                ay[:, 0:2, :].rearrange("p d v -> p (d v)"),
+                ay[:, 2:4, :].rearrange("p d v -> p (d v)"),
+                ALU.max,
+            )
+            top = work.tile([P, V], F32, name="top")
+            nc.vector.tensor_tensor(top[:], wa[:, V : 2 * V], wa[:, 2 * V : 3 * V], ALU.max)
+            root = work.tile([P, V], F32, name="root")
+            nc.scalar.activation(root[:], top[:], ACT.Abs_reciprocal_sqrt, bias=0.2)
+            nc.scalar.activation(wb[:, 2 * V : 3 * V], root[:], ACT.Square)
+            nc.scalar.activation(
+                wa[:, 0:V], top[:], ACT.Identity, bias=unit_f[:, t : t + 1], scale=unit_sb[:, t : t + 1]
+            )
+            nc.vector.scalar_tensor_tensor(
+                wb[:, V : 2 * V], zs[:, 0:V], unit_q[:, t : t + 1], wb[:, 2 * V : 3 * V], ALU.mult, ALU.mult
+            )
+            if ysum is None:
+                nc.vector.tensor_tensor(wb[:, 0:V], zs[:, V : 2 * V], wb[:, V : 2 * V], ALU.mult)
+            else:
+                nc.vector.tensor_tensor(wb[:, 0:V], ysum[:], wb[:, V : 2 * V], ALU.mult)
+            for r in range(2):
+                picks = rdr_sb[:, r * (RH // 16) : (r + 1) * (RH // 16)]
+                nc.vector.tensor_tensor(
+                    prod[r][:, t, :],
+                    wa[:].indirect(picks),
+                    qry_sb[t // 2][:, t % 2, r * RH : (r + 1) * RH],
+                    ALU.mult,
+                )
+                nc.scalar.activation(shift[r][:, t, :], wb[:].indirect(picks), ACT.Copy)
+
+        w3_bf = keep.tile([P, N * PACK], BF16, name="w3_bf", align_bytes=64)
+        nc.scalar.copy(
+            w3_bf[:].rearrange("p (c i j) -> p c j i", i=4, j=PACK),
+            w3_raw[:].rearrange("p j (c i) -> p c j i", i=4),
+        )
+        w3_codes, w3_scales = quantize(w3_bf, N, "w3")
+
+        for r in range(2):
+            hid = keep.tile([P, RH * PACK], BF16, name="hid%d" % r, align_bytes=64)
+            nc.vector.tensor_tensor(
+                hid[:].rearrange("p (c i t) -> p c t i", i=2, t=PACK),
+                prod[r][:].rearrange("p t (c i) -> p c t i", i=2),
+                shift[r][:].rearrange("p t (c i) -> p c t i", i=2),
+                ALU.add,
+            )
+            hid_codes, hid_scales = quantize(hid, RH, "hid%d" % r)
+            acc = psum.tile([P, RH], F32, name="acc", bufs=2)
+            mx(acc[:], w3_codes, w3_scales, 0, hid_codes, hid_scales, slice(0, RH), True, True)
+            res = keep.tile([P, RH], F32, name="res%d" % r)
+            nc.scalar.copy(res[:], acc[:])
+            nc.sync.dma_start(out[:, r * RH : (r + 1) * RH], res[:])

@@ -19,7 +19,13 @@ AX = mybir.AxisListType
 P = 128
 PACK = 4
 BANK = 512
-SUM_ON_PE = (2,3,)
+LIST_ROWS = 16
+FLOOR = 0.2
+HALF_H = H // 2
+HALF_U = U // 2
+FIRST_SUMMED_IN_PSUM = 2
+TILES_READ_BY_SCALAR = 2
+Y_BANKS = 4
 
 
 def tile_picked_ywvres_read_p_kernel(
@@ -29,174 +35,210 @@ def tile_picked_ywvres_read_p_kernel(
     with ExitStack() as ctx:
         lists = ctx.enter_context(tc.tile_pool(name="lists", bufs=1))
         keep = ctx.enter_context(tc.tile_pool(name="keep", bufs=1))
-        work = ctx.enter_context(tc.tile_pool(name="work", bufs=2))
         psum = ctx.enter_context(tc.psum_pool(name="psum", bufs=1))
 
-        offs_sb = lists.tile([P, S // 16], U16, name="offs_sb")
-        rdr_sb = lists.tile([P, U // 16], U16, name="rdr_sb")
-        nc.sync.dma_start(offs_sb[:], offs)
+        def sbuf(shape, dtype, name, tag=""):
+            return keep.tile(shape, dtype, name=name, tag=tag or name, align_bytes=64)
 
-        def load_half(w, c, name):
-            raw = keep.tile([P, PACK, H // 2], F32, name="%s_raw%d" % (name, c), align_bytes=64)
-            nc.sync.dma_start(
-                raw[:], w.rearrange("(p j) c -> p j c", j=PACK)[:, :, c * (H // 2) : (c + 1) * (H // 2)]
-            )
-            return raw
+        offs_sb = lists.tile([P, S // LIST_ROWS], U16, name="offs_sb")
+        rdr_sb = lists.tile([P, U // LIST_ROWS], U16, name="rdr_sb")
+        xs_all = sbuf([P, T], U8, "xs_all")
+        xw_all = sbuf([P, T], I32, "xw_all")
+        w1_raw = [sbuf([P, PACK, HALF_H], F32, "w1_raw%d" % c) for c in range(2)]
+        w2_raw = [sbuf([P, PACK, HALF_H], F32, "w2_raw%d" % c) for c in range(2)]
+        w3_raw = sbuf([P, PACK, N], F32, "w3_raw")
+        unit_sb = sbuf([P, PACK], F32, "unit_sb")
+        qry_sb = [sbuf([P, 2, U], F32, "qry%d" % c) for c in range(2)]
+        qry_rows = qry.rearrange("(p t) r -> p t r", t=PACK)
 
-        w1_raw = [load_half(w1, 0, "w1")]
-        xs_all = keep.tile([P, T], U8, name="xs_all", align_bytes=64)
+        def load_half(w, raw, c):
+            rows = w.rearrange("(p j) c -> p j c", j=PACK)
+            nc.sync.dma_start(raw[c][:], rows[:, :, c * HALF_H : (c + 1) * HALF_H])
+
         nc.vector.memset(xs_all[:].bitcast(I32), 0)
+        warm_in = sbuf([P, 1], F32, "warm_in")
+        nc.vector.memset(warm_in[:], 1.0)
+        warm_out = sbuf([P, 1], F32, "warm_out")
+        nc.scalar.activation(warm_out[:], warm_in[:], ACT.Abs_reciprocal_sqrt)
+
+        nc.sync.dma_start(offs_sb[:], offs)
+        load_half(w1, w1_raw, 0)
         for q in range(4):
             nc.sync.dma_start(
                 xs_all[32 * q : 32 * q + 4, :].bitcast(I32),
                 x_scales[0, 4 * q : 4 * q + 4, :].bitcast(I32),
             )
-        xw_all = keep.tile([P, T], I32, name="xw_all", align_bytes=64)
+        load_half(w1, w1_raw, 1)
         nc.sync.dma_start(xw_all[:], x_words[0].rearrange("p c r -> p (c r)").bitcast(I32))
-        w1_raw.append(load_half(w1, 1, "w1"))
-        w2_raw = [load_half(w2, c, "w2") for c in range(2)]
-        unit_sb = keep.tile([P, PACK], F32, name="unit_sb")
+        load_half(w2, w2_raw, 0)
+        nc.sync.dma_start(w3_raw[:], w3.rearrange("(p j) n -> p j n", j=PACK))
+        load_half(w2, w2_raw, 1)
         nc.sync.dma_start(unit_sb[:], unit.rearrange("(p t) o -> p (t o)", t=PACK))
         nc.sync.dma_start(rdr_sb[:], rdr)
-        qry_sb = []
-        for c in range(2):
-            qt = keep.tile([P, 2, U], F32, name="qry%d" % c, align_bytes=64)
-            nc.sync.dma_start(qt[:], qry.rearrange("(p t) r -> p t r", t=PACK)[:, 2 * c : 2 * c + 2, :])
-            qry_sb.append(qt)
-        w3_raw = keep.tile([P, PACK, N], F32, name="w3_raw", align_bytes=64)
-        nc.sync.dma_start(w3_raw[:], w3.rearrange("(p j) n -> p j n", j=PACK))
+        nc.sync.dma_start(qry_sb[0][:], qry_rows[:, 0:2, :])
+        nc.sync.dma_start(qry_sb[1][:], qry_rows[:, 2:4, :])
 
-        xs = keep.tile([P, S], U8, name="xs", align_bytes=64)
-        nc.vector.tensor_copy(xs[:], xs_all[:].indirect(offs_sb[:]))
-        xw = keep.tile([P, S], U32, name="xw", align_bytes=64)
-        for h in range(2):
-            nc.vector.tensor_copy(
-                xw[:, h * BANK : (h + 1) * BANK],
-                xw_all[:].bitcast(U32).indirect(offs_sb[:, h * 32 : (h + 1) * 32]),
-            )
+        xs = sbuf([P, S], U8, "xs")
+        xw = sbuf([P, S], U32, "xw")
+        xs_dealt = sbuf([P, S], U8, "xs_dealt")
+        xw_dealt = sbuf([P, S], U32, "xw_dealt")
+        w1_bf = sbuf([P, H * PACK], BF16, "w1_bf")
+        w2_bf = sbuf([P, H * PACK], BF16, "w2_bf")
+        w3_bf = sbuf([P, N * PACK], BF16, "w3_bf")
+        unit_mean = sbuf([P, PACK], F32, "unit_mean")
+        unit_floor = sbuf([P, PACK], F32, "unit_floor")
+        mag_first = sbuf([P, 2, D, V], F32, "mag_first", "w2_raw0")
+        mag = [mag_first[:, 0], mag_first[:, 1]] + [sbuf([P, D, V], F32, "mag%d" % t) for t in range(2, PACK)]
+        ysum = [sbuf([P, V], F32, "ysum%d" % t) for t in range(FIRST_SUMMED_IN_PSUM)]
+        top = [sbuf([P, V], F32, "top%d" % t) for t in range(PACK)]
+        root = [sbuf([P, V], F32, "root%d" % t) for t in range(PACK)]
+        scale_win = [sbuf([P, 3 * V], F32, "scale_win%d" % t) for t in range(PACK)]
+        shift_win = [sbuf([P, 3 * V], F32, "shift_win%d" % t) for t in range(PACK)]
+        scaled = [sbuf([P, PACK, HALF_U], F32, "scaled%d" % r) for r in range(2)]
+        shifts = [sbuf([P, PACK, HALF_U], F32, "shifts%d" % r) for r in range(2)]
+        y = {}
+        sums = {}
 
-        def round_weight(halves, name):
-            grouped = keep.tile([P, H * PACK], BF16, name=name + "_bf", align_bytes=64)
-            view = grouped[:].rearrange("p (t m j) -> p m j t", t=PACK, j=PACK)
-            for c in range(2):
-                nc.scalar.copy(
-                    view[:, c * 64 : (c + 1) * 64, :, :],
-                    halves[c][:].rearrange("p j (m t) -> p m j t", t=PACK),
-                )
-            return grouped
+        def gather_words(h):
+            picks = offs_sb[:, h * BANK // LIST_ROWS : (h + 1) * BANK // LIST_ROWS]
+            nc.vector.tensor_copy(xw[:, h * BANK : (h + 1) * BANK], xw_all[:].bitcast(U32).indirect(picks))
 
-        def quantize(grouped, width, name):
-            codes = keep.tile([P, width], U32, name=name + "_codes", align_bytes=64)
-            scales = keep.tile([P, width], U8, name=name + "_scales", align_bytes=64)
-            nc.vector.quantize_mx(out=codes[:].bitcast(FP8X4), scales=scales[:], in_=grouped[:])
+        def round_half(raw, rounded, c):
+            dealt = rounded[:].rearrange("p (t m j) -> p m j t", t=PACK, j=PACK)
+            ms = HALF_H // PACK
+            nc.scalar.copy(dealt[:, c * ms : (c + 1) * ms, :, :], raw[c][:].rearrange("p j (m t) -> p m j t", t=PACK))
+
+        def quantize(rounded, width, name):
+            codes = sbuf([P, width], U32, name + "_codes")
+            scales = sbuf([P, width], U8, name + "_scales")
+            nc.vector.quantize_mx(out=codes[:].bitcast(FP8X4), scales=scales[:], in_=rounded[:])
             return codes, scales
 
-        w1_codes, w1_scales = quantize(round_weight(w1_raw, "w1"), H, "w1")
-
-        xs_d = keep.tile([P, S], U8, name="xs_d", align_bytes=64)
-        nc.vector.tensor_copy(
-            xs_d[:].rearrange("p (d v) -> p d v", d=D), xs[:].rearrange("p (v d) -> p d v", d=D)
-        )
-        xw_d = keep.tile([P, S], U32, name="xw_d", align_bytes=64)
-        nc.vector.tensor_copy(
-            xw_d[:].rearrange("p (d c i) -> p c d i", d=D, i=4),
-            xw[:].rearrange("p (c i d) -> p c d i", d=D, i=4),
-        )
-        w2_codes, w2_scales = quantize(round_weight(w2_raw, "w2"), H, "w2")
-
-        unit_q = keep.tile([P, PACK], F32, name="unit_q")
-        nc.vector.tensor_scalar(unit_q[:], unit_sb[:], 1.0 / D, None, ALU.mult)
-        unit_f = keep.tile([P, PACK], F32, name="unit_f")
-        nc.vector.tensor_scalar(unit_f[:], unit_sb[:], 0.2, None, ALU.mult)
-
-        def mx(acc, codes, scales, t, mw, ms, cols, start, stop):
+        def mx(acc, weight, t, moving, cols, start, stop):
             nc.tensor.matmul_mx(
                 out=acc,
-                lhsT=codes[:, t * P : (t + 1) * P].bitcast(FP8X4),
-                lhsT_scale=scales[:, t * P : (t + 1) * P],
-                rhs=mw[:, cols].bitcast(FP8X4),
-                rhs_scale=ms[:, cols],
+                lhsT=weight[0][:, t * P : (t + 1) * P].bitcast(FP8X4),
+                lhsT_scale=weight[1][:, t * P : (t + 1) * P],
+                rhs=moving[0][:, cols].bitcast(FP8X4),
+                rhs_scale=moving[1][:, cols],
                 start=start,
                 stop=stop,
             )
 
-        RH = U // 2
-        prod = [keep.tile([P, PACK, RH], F32, name="prod%d" % r, align_bytes=64) for r in range(2)]
-        shift = [keep.tile([P, PACK, RH], F32, name="shift%d" % r, align_bytes=64) for r in range(2)]
+        def product(t, h):
+            bank = psum.tile([P, BANK], F32, name="y", tag="y", bufs=Y_BANKS)
+            mx(bank[:], w1_mx, t, (xw, xs), slice(h * BANK, (h + 1) * BANK), True, True)
+            y.setdefault((t, h), bank)
 
-        for t in range(PACK):
-            ay = work.tile([P, D, V], F32, name="ay")
-            ysum = None
-            if t not in SUM_ON_PE:
-                ysum = work.tile([P, V], F32, name="ysum")
-            for h in range(2):
-                y = psum.tile([P, BANK], F32, name="y", bufs=4)
-                mx(y[:], w1_codes, w1_scales, t, xw, xs, slice(h * BANK, (h + 1) * BANK), True, True)
-                nc.scalar.activation(
-                    ay[:, :, h * P : (h + 1) * P], y[:].rearrange("p (v d) -> p d v", d=D), ACT.Abs
-                )
-                if ysum is not None:
-                    nc.vector.tensor_reduce(
-                        ysum[:, h * P : (h + 1) * P], y[:].rearrange("p (v d) -> p v d", d=D), AX.X, ALU.add
-                    )
-            zs = psum.tile([P, BANK], F32, name="zs", bufs=2)
+        def magnitudes(t, h):
+            bank = y[(t, h)]
+            groups = slice(h * P, (h + 1) * P)
+            nc.scalar.activation(mag[t][:, :, groups], bank[:].rearrange("p (v d) -> p d v", d=D), ACT.Abs)
+            if t < FIRST_SUMMED_IN_PSUM:
+                nc.vector.tensor_reduce(ysum[t][:, groups], bank[:].rearrange("p (v d) -> p v d", d=D), AX.X, ALU.add)
+
+        def group_sums(t):
+            bank = psum.tile([P, BANK], F32, name="sums", tag="sums", bufs=PACK)
             for d in range(D):
-                mx(zs[:, 0:V], w2_codes, w2_scales, t, xw_d, xs_d, slice(d * V, (d + 1) * V), d == 0, d == D - 1)
-            if ysum is None:
+                mx(bank[:, 0:V], w2_mx, t, (xw_dealt, xs_dealt), slice(d * V, (d + 1) * V), d == 0, d == D - 1)
+            if t >= FIRST_SUMMED_IN_PSUM:
                 for d in range(D):
-                    mx(zs[:, V : 2 * V], w1_codes, w1_scales, t, xw_d, xs_d, slice(d * V, (d + 1) * V), d == 0, d == D - 1)
+                    mx(bank[:, V : 2 * V], w1_mx, t, (xw_dealt, xs_dealt), slice(d * V, (d + 1) * V), d == 0, d == D - 1)
+            sums.setdefault(t, bank)
 
-            wa = keep.tile([P, 3 * V], F32, name="wa%d" % t)
-            wb = keep.tile([P, 3 * V], F32, name="wb%d" % t)
+        def largest(t):
             nc.vector.tensor_tensor(
-                wa[:, V : 3 * V],
-                ay[:, 0:2, :].rearrange("p d v -> p (d v)"),
-                ay[:, 2:4, :].rearrange("p d v -> p (d v)"),
+                scale_win[t][:, V : 3 * V],
+                mag[t][:, 0:2, :].rearrange("p d v -> p (d v)"),
+                mag[t][:, 2:4, :].rearrange("p d v -> p (d v)"),
                 ALU.max,
             )
-            top = work.tile([P, V], F32, name="top")
-            nc.vector.tensor_tensor(top[:], wa[:, V : 2 * V], wa[:, 2 * V : 3 * V], ALU.max)
-            root = work.tile([P, V], F32, name="root")
-            nc.scalar.activation(root[:], top[:], ACT.Abs_reciprocal_sqrt, bias=0.2)
-            nc.scalar.activation(wb[:, 2 * V : 3 * V], root[:], ACT.Square)
-            nc.scalar.activation(
-                wa[:, 0:V], top[:], ACT.Identity, bias=unit_f[:, t : t + 1], scale=unit_sb[:, t : t + 1]
-            )
-            nc.vector.scalar_tensor_tensor(
-                wb[:, V : 2 * V], zs[:, 0:V], unit_q[:, t : t + 1], wb[:, 2 * V : 3 * V], ALU.mult, ALU.mult
-            )
-            if ysum is None:
-                nc.vector.tensor_tensor(wb[:, 0:V], zs[:, V : 2 * V], wb[:, V : 2 * V], ALU.mult)
-            else:
-                nc.vector.tensor_tensor(wb[:, 0:V], ysum[:], wb[:, V : 2 * V], ALU.mult)
-            for r in range(2):
-                picks = rdr_sb[:, r * (RH // 16) : (r + 1) * (RH // 16)]
-                nc.vector.tensor_tensor(
-                    prod[r][:, t, :],
-                    wa[:].indirect(picks),
-                    qry_sb[t // 2][:, t % 2, r * RH : (r + 1) * RH],
-                    ALU.mult,
-                )
-                nc.scalar.activation(shift[r][:, t, :], wb[:].indirect(picks), ACT.Copy)
+            nc.vector.tensor_tensor(top[t][:], scale_win[t][:, V : 2 * V], scale_win[t][:, 2 * V : 3 * V], ALU.max)
 
-        w3_bf = keep.tile([P, N * PACK], BF16, name="w3_bf", align_bytes=64)
+        def scale_terms(t):
+            nc.scalar.activation(root[t][:], top[t][:], ACT.Abs_reciprocal_sqrt, bias=FLOOR)
+            nc.scalar.activation(
+                scale_win[t][:, 0:V], top[t][:], ACT.Identity, bias=unit_floor[:, t : t + 1], scale=unit_sb[:, t : t + 1]
+            )
+            nc.scalar.activation(shift_win[t][:, 2 * V : 3 * V], root[t][:], ACT.Square)
+
+        def shift_terms(t):
+            win = shift_win[t]
+            nc.vector.scalar_tensor_tensor(
+                win[:, V : 2 * V], sums[t][:, 0:V], unit_mean[:, t : t + 1], win[:, 2 * V : 3 * V], ALU.mult, ALU.mult
+            )
+            sum_y = ysum[t][:] if t < FIRST_SUMMED_IN_PSUM else sums[t][:, V : 2 * V]
+            nc.vector.tensor_tensor(win[:, 0:V], sum_y, win[:, V : 2 * V], ALU.mult)
+
+        def read(t, r):
+            picks = rdr_sb[:, r * HALF_U // LIST_ROWS : (r + 1) * HALF_U // LIST_ROWS]
+            feats = qry_sb[t // 2][:, t % 2, r * HALF_U : (r + 1) * HALF_U]
+            if r == 0 and t < TILES_READ_BY_SCALAR:
+                fetched = sbuf([P, HALF_U], F32, "fetched%d" % t)
+                nc.scalar.activation(fetched[:], scale_win[t][:].indirect(picks), ACT.Copy)
+                nc.vector.tensor_tensor(scaled[r][:, t, :], fetched[:], feats, ALU.mult)
+            else:
+                nc.vector.tensor_tensor(scaled[r][:, t, :], scale_win[t][:].indirect(picks), feats, ALU.mult)
+            nc.scalar.activation(shifts[r][:, t, :], shift_win[t][:].indirect(picks), ACT.Copy)
+
+        nc.vector.tensor_copy(xs[:], xs_all[:].indirect(offs_sb[:]))
+        for c in range(2):
+            round_half(w1_raw, w1_bf, c)
+        w1_mx = quantize(w1_bf, H, "w1")
+        nc.gpsimd.tensor_scalar(unit_mean[:], unit_sb[:], 1.0 / D, 0.0, ALU.mult, ALU.add)
+        nc.gpsimd.tensor_scalar(unit_floor[:], unit_sb[:], FLOOR, 0.0, ALU.mult, ALU.add)
+
+        gather_words(0)
+        product(0, 0)
+        product(1, 0)
+        gather_words(1)
+        round_half(w2_raw, w2_bf, 0)
+        magnitudes(0, 0)
+        magnitudes(1, 0)
+        for t in range(2):
+            product(t, 1)
+            magnitudes(t, 1)
+        nc.vector.tensor_copy(
+            xs_dealt[:].rearrange("p (d v) -> p d v", d=D), xs[:].rearrange("p (v d) -> p d v", d=D)
+        )
+        nc.vector.tensor_copy(
+            xw_dealt[:].rearrange("p (d c i) -> p c d i", d=D, i=4),
+            xw[:].rearrange("p (c i d) -> p c d i", d=D, i=4),
+        )
+        round_half(w2_raw, w2_bf, 1)
+        w2_mx = quantize(w2_bf, H, "w2")
+
+        for t in range(PACK + 1):
+            if t < PACK:
+                largest(t)
+                if t + 2 < PACK:
+                    for h in range(2):
+                        product(t + 2, h)
+                        magnitudes(t + 2, h)
+                group_sums(t)
+                scale_terms(t)
+            if t >= 1:
+                shift_terms(t - 1)
+
         nc.scalar.copy(
             w3_bf[:].rearrange("p (c i j) -> p c j i", i=4, j=PACK),
             w3_raw[:].rearrange("p j (c i) -> p c j i", i=4),
         )
-        w3_codes, w3_scales = quantize(w3_bf, N, "w3")
+        w3_mx = quantize(w3_bf, N, "w3")
 
         for r in range(2):
-            hid = keep.tile([P, RH * PACK], BF16, name="hid%d" % r, align_bytes=64)
+            for t in range(PACK):
+                read(t, r)
+            hid = sbuf([P, HALF_U * PACK], BF16, "hid%d" % r)
             nc.vector.tensor_tensor(
                 hid[:].rearrange("p (c i t) -> p c t i", i=2, t=PACK),
-                prod[r][:].rearrange("p t (c i) -> p c t i", i=2),
-                shift[r][:].rearrange("p t (c i) -> p c t i", i=2),
+                scaled[r][:].rearrange("p t (c i) -> p c t i", i=2),
+                shifts[r][:].rearrange("p t (c i) -> p c t i", i=2),
                 ALU.add,
             )
-            hid_codes, hid_scales = quantize(hid, RH, "hid%d" % r)
-            acc = psum.tile([P, RH], F32, name="acc", bufs=2)
-            mx(acc[:], w3_codes, w3_scales, 0, hid_codes, hid_scales, slice(0, RH), True, True)
-            res = keep.tile([P, RH], F32, name="res%d" % r)
+            hid_mx = quantize(hid, HALF_U, "hid%d" % r)
+            acc = psum.tile([P, HALF_U], F32, name="acc", tag="y", bufs=Y_BANKS)
+            mx(acc[:], w3_mx, 0, hid_mx, slice(0, HALF_U), True, True)
+            res = sbuf([P, HALF_U], F32, "res%d" % r)
             nc.scalar.copy(res[:], acc[:])
-            nc.sync.dma_start(out[:, r * RH : (r + 1) * RH], res[:])
+            nc.sync.dma_start(out[:, r * HALF_U : (r + 1) * HALF_U], res[:])

@@ -24,7 +24,6 @@ FLOOR = 0.2
 HALF_H = H // 2
 HALF_U = U // 2
 FIRST_SUMMED_IN_PSUM = 2
-TILES_READ_BY_SCALAR = 2
 Y_BANKS = 4
 
 
@@ -132,7 +131,7 @@ def tile_picked_ywvres_read_p_kernel(
 
         def magnitudes(t, h):
             bank = y[(t, h)]
-            groups = slice(h * P, (h + 1) * P)
+            groups = slice(h * BANK // D, (h + 1) * BANK // D)
             nc.scalar.activation(mag[t][:, :, groups], bank[:].rearrange("p (v d) -> p d v", d=D), ACT.Abs)
             if t < FIRST_SUMMED_IN_PSUM:
                 nc.vector.tensor_reduce(ysum[t][:, groups], bank[:].rearrange("p (v d) -> p v d", d=D), AX.X, ALU.add)
@@ -173,12 +172,7 @@ def tile_picked_ywvres_read_p_kernel(
         def read(t, r):
             picks = rdr_sb[:, r * HALF_U // LIST_ROWS : (r + 1) * HALF_U // LIST_ROWS]
             feats = qry_sb[t // 2][:, t % 2, r * HALF_U : (r + 1) * HALF_U]
-            if r == 0 and t < TILES_READ_BY_SCALAR:
-                fetched = sbuf([P, HALF_U], F32, "fetched%d" % t)
-                nc.scalar.activation(fetched[:], scale_win[t][:].indirect(picks), ACT.Copy)
-                nc.vector.tensor_tensor(scaled[r][:, t, :], fetched[:], feats, ALU.mult)
-            else:
-                nc.vector.tensor_tensor(scaled[r][:, t, :], scale_win[t][:].indirect(picks), feats, ALU.mult)
+            nc.vector.tensor_tensor(scaled[r][:, t, :], scale_win[t][:].indirect(picks), feats, ALU.mult)
             nc.scalar.activation(shifts[r][:, t, :], shift_win[t][:].indirect(picks), ACT.Copy)
 
         nc.vector.tensor_copy(xs[:], xs_all[:].indirect(offs_sb[:]))

from contextlib import ExitStack

import concourse.mybir as mybir

K, T, S, D, N, H, V, U = 512, 2048, 1024, 4, 128, 512, 256, 512
FLOPS = 2 * K * H * S * 2 + 2 * H * N * U

F32 = mybir.dt.float32
BF16 = mybir.dt.bfloat16
I32 = mybir.dt.int32
U32 = mybir.dt.uint32
U16 = mybir.dt.uint16
U8 = mybir.dt.uint8
FP8X4 = mybir.dt.float8_e4m3fn_x4
ALU = mybir.AluOpType
ACT = mybir.ActivationFunctionType
AX = mybir.AxisListType

P = 128
PACK = 4
BANK = 512
LIST_ROWS = 16
FLOOR = 0.2
HALF_H = H // 2
HALF_U = U // 2
FIRST_SUMMED_IN_PSUM = 2
Y_BANKS = 4


def tile_picked_ywvres_read_p_kernel(
    tc, x_words, x_scales, w1, w2, qry, unit, w3, offs, rdr, out
):
    nc = tc.nc
    with ExitStack() as ctx:
        lists = ctx.enter_context(tc.tile_pool(name="lists", bufs=1))
        keep = ctx.enter_context(tc.tile_pool(name="keep", bufs=1))
        psum = ctx.enter_context(tc.psum_pool(name="psum", bufs=1))

        def sbuf(shape, dtype, name, tag=""):
            return keep.tile(shape, dtype, name=name, tag=tag or name, align_bytes=64)

        offs_sb = lists.tile([P, S // LIST_ROWS], U16, name="offs_sb")
        rdr_sb = lists.tile([P, U // LIST_ROWS], U16, name="rdr_sb")
        xs_all = sbuf([P, T], U8, "xs_all")
        xw_all = sbuf([P, T], I32, "xw_all")
        w1_raw = [sbuf([P, PACK, HALF_H], F32, "w1_raw%d" % c) for c in range(2)]
        w2_raw = [sbuf([P, PACK, HALF_H], F32, "w2_raw%d" % c) for c in range(2)]
        w3_raw = sbuf([P, PACK, N], F32, "w3_raw")
        unit_sb = sbuf([P, PACK], F32, "unit_sb")
        qry_sb = [sbuf([P, 2, U], F32, "qry%d" % c) for c in range(2)]
        qry_rows = qry.rearrange("(p t) r -> p t r", t=PACK)

        def load_half(w, raw, c):
            rows = w.rearrange("(p j) c -> p j c", j=PACK)
            nc.sync.dma_start(raw[c][:], rows[:, :, c * HALF_H : (c + 1) * HALF_H])

        nc.vector.memset(xs_all[:].bitcast(I32), 0)
        warm_in = sbuf([P, 1], F32, "warm_in")
        nc.vector.memset(warm_in[:], 1.0)
        warm_out = sbuf([P, 1], F32, "warm_out")
        nc.scalar.activation(warm_out[:], warm_in[:], ACT.Abs_reciprocal_sqrt)

        nc.sync.dma_start(offs_sb[:], offs)
        load_half(w1, w1_raw, 0)
        for q in range(4):
            nc.sync.dma_start(
                xs_all[32 * q : 32 * q + 4, :].bitcast(I32),
                x_scales[0, 4 * q : 4 * q + 4, :].bitcast(I32),
            )
        load_half(w1, w1_raw, 1)
        nc.sync.dma_start(xw_all[:], x_words[0].rearrange("p c r -> p (c r)").bitcast(I32))
        load_half(w2, w2_raw, 0)
        nc.sync.dma_start(w3_raw[:], w3.rearrange("(p j) n -> p j n", j=PACK))
        load_half(w2, w2_raw, 1)
        nc.sync.dma_start(unit_sb[:], unit.rearrange("(p t) o -> p (t o)", t=PACK))
        nc.sync.dma_start(rdr_sb[:], rdr)
        nc.sync.dma_start(qry_sb[0][:], qry_rows[:, 0:2, :])
        nc.sync.dma_start(qry_sb[1][:], qry_rows[:, 2:4, :])

        xs = sbuf([P, S], U8, "xs")
        xw = sbuf([P, S], U32, "xw")
        xs_dealt = sbuf([P, S], U8, "xs_dealt")
        xw_dealt = sbuf([P, S], U32, "xw_dealt")
        w1_bf = sbuf([P, H * PACK], BF16, "w1_bf")
        w2_bf = sbuf([P, H * PACK], BF16, "w2_bf")
        w3_bf = sbuf([P, N * PACK], BF16, "w3_bf")
        unit_mean = sbuf([P, PACK], F32, "unit_mean")
        unit_floor = sbuf([P, PACK], F32, "unit_floor")
        mag_first = sbuf([P, 2, D, V], F32, "mag_first", "w2_raw0")
        mag = [mag_first[:, 0], mag_first[:, 1]] + [sbuf([P, D, V], F32, "mag%d" % t) for t in range(2, PACK)]
        ysum = [sbuf([P, V], F32, "ysum%d" % t) for t in range(FIRST_SUMMED_IN_PSUM)]
        top = [sbuf([P, V], F32, "top%d" % t) for t in range(PACK)]
        root = [sbuf([P, V], F32, "root%d" % t) for t in range(PACK)]
        scale_win = [sbuf([P, 3 * V], F32, "scale_win%d" % t) for t in range(PACK)]
        shift_win = [sbuf([P, 3 * V], F32, "shift_win%d" % t) for t in range(PACK)]
        scaled = [sbuf([P, PACK, HALF_U], F32, "scaled%d" % r) for r in range(2)]
        shifts = [sbuf([P, PACK, HALF_U], F32, "shifts%d" % r) for r in range(2)]
        y = {}
        sums = {}

        def gather_words(h):
            picks = offs_sb[:, h * BANK // LIST_ROWS : (h + 1) * BANK // LIST_ROWS]
            nc.vector.tensor_copy(xw[:, h * BANK : (h + 1) * BANK], xw_all[:].bitcast(U32).indirect(picks))

        def round_half(raw, rounded, c):
            dealt = rounded[:].rearrange("p (t m j) -> p m j t", t=PACK, j=PACK)
            ms = HALF_H // PACK
            nc.scalar.copy(dealt[:, c * ms : (c + 1) * ms, :, :], raw[c][:].rearrange("p j (m t) -> p m j t", t=PACK))

        def quantize(rounded, width, name):
            codes = sbuf([P, width], U32, name + "_codes")
            scales = sbuf([P, width], U8, name + "_scales")
            nc.vector.quantize_mx(out=codes[:].bitcast(FP8X4), scales=scales[:], in_=rounded[:])
            return codes, scales

        def mx(acc, weight, t, moving, cols, start, stop):
            nc.tensor.matmul_mx(
                out=acc,
                lhsT=weight[0][:, t * P : (t + 1) * P].bitcast(FP8X4),
                lhsT_scale=weight[1][:, t * P : (t + 1) * P],
                rhs=moving[0][:, cols].bitcast(FP8X4),
                rhs_scale=moving[1][:, cols],
                start=start,
                stop=stop,
            )

        def product(t, h):
            bank = psum.tile([P, BANK], F32, name="y", tag="y", bufs=Y_BANKS)
            mx(bank[:], w1_mx, t, (xw, xs), slice(h * BANK, (h + 1) * BANK), True, True)
            y.setdefault((t, h), bank)

        def magnitudes(t, h):
            bank = y[(t, h)]
            groups = slice(h * BANK // D, (h + 1) * BANK // D)
            nc.scalar.activation(mag[t][:, :, groups], bank[:].rearrange("p (v d) -> p d v", d=D), ACT.Abs)
            if t < FIRST_SUMMED_IN_PSUM:
                nc.vector.tensor_reduce(ysum[t][:, groups], bank[:].rearrange("p (v d) -> p v d", d=D), AX.X, ALU.add)

        def group_sums(t):
            bank = psum.tile([P, BANK], F32, name="sums", tag="sums", bufs=PACK)
            for d in range(D):
                mx(bank[:, 0:V], w2_mx, t, (xw_dealt, xs_dealt), slice(d * V, (d + 1) * V), d == 0, d == D - 1)
            if t >= FIRST_SUMMED_IN_PSUM:
                for d in range(D):
                    mx(bank[:, V : 2 * V], w1_mx, t, (xw_dealt, xs_dealt), slice(d * V, (d + 1) * V), d == 0, d == D - 1)
            sums.setdefault(t, bank)

        def largest(t):
            nc.vector.tensor_tensor(
                scale_win[t][:, V : 3 * V],
                mag[t][:, 0:2, :].rearrange("p d v -> p (d v)"),
                mag[t][:, 2:4, :].rearrange("p d v -> p (d v)"),
                ALU.max,
            )
            nc.vector.tensor_tensor(top[t][:], scale_win[t][:, V : 2 * V], scale_win[t][:, 2 * V : 3 * V], ALU.max)

        def scale_terms(t):
            nc.scalar.activation(root[t][:], top[t][:], ACT.Abs_reciprocal_sqrt, bias=FLOOR)
            nc.scalar.activation(
                scale_win[t][:, 0:V], top[t][:], ACT.Identity, bias=unit_floor[:, t : t + 1], scale=unit_sb[:, t : t + 1]
            )
            nc.scalar.activation(shift_win[t][:, 2 * V : 3 * V], root[t][:], ACT.Square)

        def shift_terms(t):
            win = shift_win[t]
            nc.vector.scalar_tensor_tensor(
                win[:, V : 2 * V], sums[t][:, 0:V], unit_mean[:, t : t + 1], win[:, 2 * V : 3 * V], ALU.mult, ALU.mult
            )
            sum_y = ysum[t][:] if t < FIRST_SUMMED_IN_PSUM else sums[t][:, V : 2 * V]
            nc.vector.tensor_tensor(win[:, 0:V], sum_y, win[:, V : 2 * V], ALU.mult)

        def read(t, r):
            picks = rdr_sb[:, r * HALF_U // LIST_ROWS : (r + 1) * HALF_U // LIST_ROWS]
            feats = qry_sb[t // 2][:, t % 2, r * HALF_U : (r + 1) * HALF_U]
            nc.vector.tensor_tensor(scaled[r][:, t, :], scale_win[t][:].indirect(picks), feats, ALU.mult)
            nc.scalar.activation(shifts[r][:, t, :], shift_win[t][:].indirect(picks), ACT.Copy)

        nc.vector.tensor_copy(xs[:], xs_all[:].indirect(offs_sb[:]))
        for c in range(2):
            round_half(w1_raw, w1_bf, c)
        w1_mx = quantize(w1_bf, H, "w1")
        nc.gpsimd.tensor_scalar(unit_mean[:], unit_sb[:], 1.0 / D, 0.0, ALU.mult, ALU.add)
        nc.gpsimd.tensor_scalar(unit_floor[:], unit_sb[:], FLOOR, 0.0, ALU.mult, ALU.add)

        gather_words(0)
        product(0, 0)
        product(1, 0)
        gather_words(1)
        round_half(w2_raw, w2_bf, 0)
        magnitudes(0, 0)
        magnitudes(1, 0)
        for t in range(2):
            product(t, 1)
            magnitudes(t, 1)
        nc.vector.tensor_copy(
            xs_dealt[:].rearrange("p (d v) -> p d v", d=D), xs[:].rearrange("p (v d) -> p d v", d=D)
        )
        nc.vector.tensor_copy(
            xw_dealt[:].rearrange("p (d c i) -> p c d i", d=D, i=4),
            xw[:].rearrange("p (c i d) -> p c d i", d=D, i=4),
        )
        round_half(w2_raw, w2_bf, 1)
        w2_mx = quantize(w2_bf, H, "w2")

        for t in range(PACK + 1):
            if t < PACK:
                largest(t)
                if t + 2 < PACK:
                    for h in range(2):
                        product(t + 2, h)
                        magnitudes(t + 2, h)
                group_sums(t)
                scale_terms(t)
            if t >= 1:
                shift_terms(t - 1)

        nc.scalar.copy(
            w3_bf[:].rearrange("p (c i j) -> p c j i", i=4, j=PACK),
            w3_raw[:].rearrange("p j (c i) -> p c j i", i=4),
        )
        w3_mx = quantize(w3_bf, N, "w3")

        for r in range(2):
            for t in range(PACK):
                read(t, r)
            hid = sbuf([P, HALF_U * PACK], BF16, "hid%d" % r)
            nc.vector.tensor_tensor(
                hid[:].rearrange("p (c i t) -> p c t i", i=2, t=PACK),
                scaled[r][:].rearrange("p t (c i) -> p c t i", i=2),
                shifts[r][:].rearrange("p t (c i) -> p c t i", i=2),
                ALU.add,
            )
            hid_mx = quantize(hid, HALF_U, "hid%d" % r)
            acc = psum.tile([P, HALF_U], F32, name="acc", tag="y", bufs=Y_BANKS)
            mx(acc[:], w3_mx, 0, hid_mx, slice(0, HALF_U), True, True)
            res = sbuf([P, HALF_U], F32, "res%d" % r)
            nc.scalar.copy(res[:], acc[:])
            nc.sync.dma_start(out[:, r * HALF_U : (r + 1) * HALF_U], res[:])
